import numpy as np
import ml_dtypes


def mxq(x, axis, fmt="e4m3"):
    dtype, down = {"e4m3": (ml_dtypes.float8_e4m3fn, 7), "e5m2": (ml_dtypes.float8_e5m2, 14)}[fmt]
    v = np.moveaxis(np.asarray(x, np.float32).astype(ml_dtypes.bfloat16).astype(np.float64), axis, -1)
    blocks = v.reshape(v.shape[:-1] + (-1, 32))
    amax = np.abs(blocks).max(-1, keepdims=True)
    byte = np.maximum(np.where(amax > 0, np.frexp(amax)[1] - 1 + 127, 0) - down, 1)
    scale = np.exp2(byte - 127.0)
    codes = (blocks / scale).astype(np.float32).astype(dtype).astype(np.float64)
    return np.moveaxis((codes * scale).reshape(v.shape), -1, axis)


WIDE = False


def mx_kscale(k):
    if not WIDE:
        return np.ones(k)
    levels = np.array([30, -30])
    if k % 512:
        return np.exp2(np.random.permutation(np.resize(levels, k // 32))).repeat(32)
    a = np.empty((k // 512, 16))
    for p in range(k // 512):
        a[p, :8] = np.random.permutation(np.resize(levels, 8))
        for g in range(8):
            far = levels[np.abs(levels - a[p, g]) >= 10]
            a[p, g + 8] = far[np.random.randint(len(far))]
    return np.exp2(a.ravel()).repeat(32)


def f64(x):
    return np.asarray(x).astype(np.float64)


def striped(idx):
    return np.tile(np.asarray(idx).reshape(-1, 16).T, (8, 1)).astype(np.uint16)


def unstriped(offs):
    return offs[:16].T.reshape(-1).astype(np.int64)


def striped8(idx):
    return np.asarray(idx).reshape(8, -1, 16).transpose(0, 2, 1).reshape(128, -1).astype(np.uint16)


def unstriped8(offs):
    return offs.reshape(8, 16, -1).transpose(0, 2, 1).reshape(8, -1).astype(np.int64)


def pick8(x, idx, run):
    r = np.arange(len(x))
    return x[r[:, None], idx[r % (8 * run) // run]]


E2M1 = np.array([0.0, 0.5, 1.0, 1.5, 2.0, 3.0, 4.0, 6.0, -0.0, -0.5, -1.0, -1.5, -2.0, -3.0, -4.0, -6.0])


def pack_weight(w, fmt):
    k, n = w.shape
    w = f64(np.asarray(w, np.float32).astype(ml_dtypes.bfloat16)).reshape(k // 32, 32, n)
    amax = np.abs(w).max(1)
    if fmt in ("e4m3", "e5m2"):
        byte = np.frexp(amax)[1] - 1 + 127 - (7 if fmt == "e4m3" else 14)
    else:
        mant, ex = np.frexp(amax / 6.0)
        byte = np.where(mant > 0.5, ex, ex - 1) + 127
    byte = np.clip(np.where(amax > 0, byte, 1), 1, 254)
    scaled = (w * np.exp2(127.0 - byte)[:, None, :]).reshape(k, n).astype(np.float32)
    by_word = np.ascontiguousarray(scaled.reshape(k // 512, 128, 4, n).transpose(0, 1, 3, 2))
    if fmt in ("e4m3", "e5m2"):
        words = by_word.astype(ml_dtypes.float8_e4m3fn if fmt == "e4m3" else ml_dtypes.float8_e5m2).view(np.uint8)
    else:
        c = by_word.astype(ml_dtypes.float4_e2m1fn).view(np.uint8) & 0xF
        words = (c[..., 0::2] | (c[..., 1::2] << 4)).reshape(k // 512, 128, 2 * n)
    return np.ascontiguousarray(words), np.ascontiguousarray(byte.astype(np.uint8).reshape(k // 512, 16, n))


def unpack_weight(words, scales, fmt):
    g, _, n = scales.shape
    words = np.ascontiguousarray(words).reshape(g, 128, n, -1)
    if fmt in ("e4m3", "e5m2"):
        vals = words.view(ml_dtypes.float8_e4m3fn if fmt == "e4m3" else ml_dtypes.float8_e5m2).astype(np.float64)
    else:
        nib = np.empty((g, 128, n, 4), np.uint8)
        nib[..., 0::2] = words & 0xF
        nib[..., 1::2] = words >> 4
        vals = E2M1[nib]
    vals = vals * np.repeat(np.exp2(scales.astype(np.float64) - 127.0), 8, axis=1)[..., None]
    return vals.transpose(0, 1, 3, 2).reshape(g * 512, n)


K, T, J, R, C, O, U, D, N, E = 512, 1024, 256, 512, 512, 128, 128, 256, 256, 1024


def setup_inputs():
    n = np.random.standard_normal
    idx = np.random.permutation(T)[:J]
    idx2 = np.stack([np.random.permutation(C)[:J] for _ in range(8)])
    idx3 = np.random.permutation(C)[:O]
    idx4 = np.random.permutation(C)[:U]
    idx5 = np.random.permutation(T)[:D]
    idx6 = np.random.permutation(E)[:D]
    fk = mx_kscale(K)
    fr = mx_kscale(R)
    xtp = pack_weight(n((K, T)) / fk[:, None], "e2m1")
    wp = pack_weight(n((K, R)) * 1 / np.sqrt(K) * fk[:, None] * fr, "e5m2")
    wbp = pack_weight(n((R, N)) * 1 / np.sqrt(R) / fr[:, None], "e4m3")
    wsp = pack_weight(n((K, N)) * 1 / np.sqrt(K) * fk[:, None], "e4m3")
    return {
        "xt_words": xtp[0],
        "xt_scales": xtp[1],
        "w_words": wp[0],
        "w_scales": wp[1],
        "sa": (np.random.uniform(0.5, 1.6, (R, 1))).astype(np.float32),
        "sb": (np.random.uniform(0.5, 1.6, (R, 1))).astype(np.float32),
        "wb_words": wbp[0],
        "wb_scales": wbp[1],
        "ws_words": wsp[0],
        "ws_scales": wsp[1],
        "offs": striped(idx),
        "offs2": striped8(idx2),
        "offs3": striped(idx3),
        "offs4": striped(idx4),
        "offs5": striped(idx5),
        "offs6": striped(idx6),
    }


def reference(xt_words, xt_scales, w_words, w_scales, sa, sb, wb_words, wb_scales, ws_words, ws_scales, offs, offs2, offs3, offs4, offs5, offs6):
    idx = unstriped(offs)
    idx2 = unstriped8(offs2)
    idx3 = unstriped(offs3)
    idx4 = unstriped(offs4)
    idx5 = unstriped(offs5)
    idx6 = unstriped(offs6)
    xtu = unpack_weight(xt_words, xt_scales, "e2m1")
    wu = unpack_weight(w_words, w_scales, "e5m2")
    wbu = unpack_weight(wb_words, wb_scales, "e4m3")
    wsu = unpack_weight(ws_words, ws_scales, "e4m3")
    xtidxg = xtu[:, idx]
    a = wu.T @ xtidxg
    pw = np.zeros((R, C))
    pw[np.arange(R)[:, None], idx2[np.arange(R) % 512 // 64]] = a
    h1 = pw[:, idx3] * f64(sa)
    h2 = pw[:, idx4] * f64(sb)
    hid = np.concatenate([h1, h2], axis=1)
    hidq = mxq(hid, 0, "e5m2")
    xtidx5g = xtu[:, idx5]
    p = wbu.T @ hidq + wsu.T @ xtidx5g
    y = np.zeros((N, E))
    y[:, idx6] = p
    return y

@@ -1,0 +1,190 @@
+from contextlib import ExitStack
+
+import concourse.mybir as mybir
+
+K, T, J, R, C, O, U, D, N, E = 512, 1024, 256, 512, 512, 128, 128, 256, 256, 1024
+FLOPS = 2 * K * R * J + 2 * R * N * D + 2 * K * N * D
+
+F32 = mybir.dt.float32
+BF16 = mybir.dt.bfloat16
+I32 = mybir.dt.int32
+U32 = mybir.dt.uint32
+U16 = mybir.dt.uint16
+U8 = mybir.dt.uint8
+E4M3 = mybir.dt.float8_e4m3fn_x4
+E5M2 = mybir.dt.float8_e5m2_x4
+E2M1 = mybir.dt.float4_e2m1fn_x4
+COPY = mybir.ActivationFunctionType.Copy
+
+P = 128
+PACK = 4
+QUADS = 4
+HALF = 128
+PER_COL = 16
+
+
+def tile_list_ownsides_solo_further_scattered_kernel(
+    tc, xt_words, xt_scales, w_words, w_scales, sa, sb, wb_words, wb_scales, ws_words, ws_scales,
+    offs, offs2, offs3, offs4, offs5, offs6, out,
+):
+    nc = tc.nc
+    with ExitStack() as ctx:
+        lists = ctx.enter_context(tc.tile_pool(name="lists", bufs=1))
+        keep = ctx.enter_context(tc.tile_pool(name="keep", bufs=1))
+        psum = ctx.enter_context(tc.psum_pool(name="psum", bufs=1))
+
+        def sb_tile(shape, dtype, name, tag=None):
+            return keep.tile(shape, dtype, name=name, tag=tag or name, align_bytes=64)
+
+        def load_list(src, name):
+            dst = lists.tile(list(src.shape), U16, name=name)
+            nc.sync.dma_start(dst[:], src)
+            return dst
+
+        def load_words(src, name, tag=None):
+            dst = sb_tile([P, src.shape[2]], U32, name, tag)
+            nc.sync.dma_start(dst[:].bitcast(I32), src[0].rearrange("p n t -> p (n t)").bitcast(I32))
+            return dst
+
+        def zeroed_plane(width, name, tag=None):
+            plane = sb_tile([P, width], U8, name, tag)
+            nc.vector.memset(plane[:].bitcast(I32), 0)
+            return plane
+
+        def load_plane(plane, src):
+            for q in range(QUADS):
+                nc.sync.dma_start(plane[32 * q : 32 * q + 4, :].bitcast(I32), src[0, 4 * q : 4 * q + 4, :].bitcast(I32))
+
+        def list_half(tile, h):
+            return tile[:, h * HALF // PER_COL : (h + 1) * HALF // PER_COL]
+
+        xt_plane = zeroed_plane(T, "xt_plane")
+        w_plane = zeroed_plane(R, "w_plane", "w_plane_board3")
+
+        w_stage = sb_tile([4, QUADS, R // 4], I32, "w_stage")
+        nc.sync.dma_start(w_stage[:], w_scales[0].bitcast(I32).rearrange("(q r) c -> r q c", r=4))
+        idx = load_list(offs, "idx")
+        xt_table = sb_tile([P, T], U16, "xt_table")
+        nc.sync.dma_start(xt_table[:].bitcast(I32), xt_words[0].bitcast(I32))
+        w_raw = load_words(w_words, "w_raw", "w_raw_board2")
+        load_plane(xt_plane, xt_scales)
+        idx2 = load_list(offs2, "idx2")
+
+        boards = [sb_tile([P, C], F32, "board0"), sb_tile([P, C], F32, "board1")]
+        for board in boards:
+            nc.vector.memset(board[:], 0.0)
+
+        for q in range(QUADS):
+            nc.vector.tensor_copy(w_plane[32 * q : 32 * q + 4, :].bitcast(I32), w_stage[0:4, q, :])
+
+        w_codes, w_bytes = [], []
+
+        def deal_w(pair):
+            codes = sb_tile([P, 2, P], U32, "w_codes%d" % pair)
+            nc.scalar.copy(
+                codes[:].rearrange("p t m -> p m t"),
+                w_raw[:].rearrange("p (m t) -> p m t", t=PACK)[:, :, 2 * pair : 2 * pair + 2],
+            )
+            scales = sb_tile([P, 2, P], U8, "w_bytes%d" % pair)
+            nc.vector.tensor_copy(
+                scales[:], w_plane[:].rearrange("p (m t) -> p t m", t=PACK)[:, 2 * pair : 2 * pair + 2, :]
+            )
+            w_codes.extend([codes[:, 0, :], codes[:, 1, :]])
+            w_bytes.extend([scales[:, 0, :], scales[:, 1, :]])
+
+        slot_words = sb_tile([P, J], U16, "slot_words")
+        slot_bytes = sb_tile([P, J], U8, "slot_bytes")
+        hidden = [sb_tile([P, J], F32, "hidden%d" % t, "hidden%d_next" % t) for t in range(PACK)]
+
+        def gather_slots(h):
+            cols = slice(h * HALF, (h + 1) * HALF)
+            nc.vector.tensor_copy(slot_words[:, cols], xt_table[:].indirect(list_half(idx, h)))
+            nc.vector.tensor_copy(slot_bytes[:, cols], xt_plane[:].indirect(list_half(idx, h)))
+
+        def first_stage(t, cols, offsets, bank):
+            acc = psum.tile([P, cols.stop - cols.start], F32, name="acc_a%d_%d" % (t, cols.start), tag=bank)
+            nc.tensor.matmul_mx(
+                acc[:], lhsT=w_codes[t].bitcast(E5M2), lhsT_scale=w_bytes[t],
+                rhs=slot_words[:, cols].bitcast(E2M1), rhs_scale=slot_bytes[:, cols], start=True, stop=True,
+            )
+            nc.vector.tensor_copy(hidden[t][:, cols], acc[:])
+            nc.scalar.activation(boards[t][:].indirect(offsets), hidden[t][:, cols], COPY)
+
+        deal_w(0)
+        for h in range(2):
+            gather_slots(h)
+            for t in range(2):
+                first_stage(t, slice(h * HALF, (h + 1) * HALF), list_half(idx2, h), "bank%d" % (2 * h + t))
+        deal_w(1)
+        boards.append(sb_tile([P, C], F32, "board2", "w_raw_board2"))
+        boards.append(sb_tile([P, C], F32, "board3", "w_plane_board3"))
+        for t in range(2, PACK):
+            nc.gpsimd.memset(boards[t][:], 0.0)
+            first_stage(t, slice(0, J), idx2[:], "bank%d" % (2 + t))
+
+        idx3 = load_list(offs3, "idx3")
+        sa_t = sb_tile([P, PACK], F32, "sa_t", "sa_picked1")
+        nc.sync.dma_start(sa_t[:], sa.rearrange("(p t) o -> p (t o)", t=PACK))
+        idx5 = load_list(offs5, "idx5")
+        ws_codes = load_words(ws_words, "ws_codes")
+        ws_plane = zeroed_plane(N, "ws_plane")
+        load_plane(ws_plane, ws_scales)
+        idx4 = load_list(offs4, "idx4")
+        sb_t = sb_tile([P, PACK], F32, "sb_t")
+        nc.sync.dma_start(sb_t[:], sb.rearrange("(p t) o -> p (t o)", t=PACK))
+        wb_codes = load_words(wb_words, "wb_codes")
+        wb_plane = zeroed_plane(N, "wb_plane")
+        load_plane(wb_plane, wb_scales)
+        idx6 = load_list(offs6, "idx6")
+
+        short_words = sb_tile([P, D], U16, "short_words")
+        short_bytes = sb_tile([P, D], U8, "short_bytes")
+        nc.vector.tensor_copy(short_words[:], xt_table[:].indirect(idx5[:]))
+        nc.vector.tensor_copy(short_bytes[:], xt_plane[:].indirect(idx5[:]))
+
+        sums = {}
+        for h in range(2):
+            cols = slice(h * HALF, (h + 1) * HALF)
+            for n in range(N // P):
+                rows = slice(n * P, (n + 1) * P)
+                sums[h, n] = psum.tile([P, HALF], F32, name="acc_p%d_%d" % (h, n), tag="bank%d" % (2 * h + n))
+                nc.tensor.matmul_mx(
+                    sums[h, n][:], lhsT=ws_codes[:, rows].bitcast(E4M3), lhsT_scale=ws_plane[:, rows],
+                    rhs=short_words[:, cols].bitcast(E2M1), rhs_scale=short_bytes[:, cols], start=True, stop=False,
+                )
+
+        pages = []
+        for n in range(N // P):
+            pages.append(sb_tile([P, E], F32, "page%d" % n, "hidden%d_next" % n))
+            nc.gpsimd.memset(pages[n][:], 0.0)
+
+        picked = [sb_tile([P, PACK, HALF], BF16, "picked0"), sb_tile([P, PACK, HALF], BF16, "picked1", "sa_picked1")]
+        for h, (places, weight) in enumerate(((idx3, sa_t), (idx4, sb_t))):
+            for t in range(PACK):
+                nc.scalar.activation(
+                    picked[h][:, t, :], boards[t][:].indirect(places[:]), COPY, scale=weight[:, t : t + 1]
+                )
+
+        for h in range(2):
+            woven = sb_tile([P, HALF, PACK], BF16, "woven%d" % h, "woven")
+            nc.vector.tensor_copy(woven[:], picked[h][:].rearrange("p t d -> p d t"))
+            hid_codes = sb_tile([P, HALF], U32, "hid_codes%d" % h)
+            hid_bytes = sb_tile([P, HALF], U8, "hid_bytes%d" % h)
+            nc.vector.quantize_mx(hid_codes[:].bitcast(E5M2), hid_bytes[:], woven[:].rearrange("p d t -> p (d t)"))
+            for n in range(N // P):
+                rows = slice(n * P, (n + 1) * P)
+                nc.tensor.matmul_mx(
+                    sums[h, n][:], lhsT=wb_codes[:, rows].bitcast(E4M3), lhsT_scale=wb_plane[:, rows],
+                    rhs=hid_codes[:].bitcast(E5M2), rhs_scale=hid_bytes[:], start=False, stop=True,
+                )
+
+        for h in range(2):
+            result0 = sb_tile([P, HALF], F32, "result0_%d" % h)
+            nc.scalar.copy(result0[:], sums[h, 0][:])
+            nc.scalar.activation(pages[0][:].indirect(list_half(idx6, h)), result0[:], COPY)
+            result1 = sb_tile([P, HALF], F32, "result1_%d" % h)
+            nc.vector.tensor_copy(result1[:], sums[h, 1][:])
+            nc.vector.tensor_copy(pages[1][:].indirect(list_half(idx6, h)), result1[:])
+
+        nc.scalar.dma_start(out[0:P, :], pages[0][:])
+        nc.sync.dma_start(out[P : 2 * P, :], pages[1][:])

@@ -41,14 +41,14 @@ def tile_list_ownsides_solo_further_scattered_kernel(
             nc.sync.dma_start(dst[:], src)
             return dst
 
-        def load_words(src, name, tag=None):
-            dst = sb_tile([P, src.shape[2]], U32, name, tag)
-            nc.sync.dma_start(dst[:].bitcast(I32), src[0].rearrange("p n t -> p (n t)").bitcast(I32))
+        def load_words(src, name, queue):
+            dst = sb_tile([P, src.shape[2]], U32, name)
+            queue.dma_start(dst[:].bitcast(I32), src[0].rearrange("p n t -> p (n t)").bitcast(I32))
             return dst
 
-        def zeroed_plane(width, name, tag=None):
-            plane = sb_tile([P, width], U8, name, tag)
-            nc.vector.memset(plane[:].bitcast(I32), 0)
+        def zeroed_plane(width, name, engine):
+            plane = sb_tile([P, width], U8, name)
+            engine.memset(plane[:].bitcast(I32), 0)
             return plane
 
         def load_plane(plane, src):
@@ -58,15 +58,15 @@ def tile_list_ownsides_solo_further_scattered_kernel(
         def list_half(tile, h):
             return tile[:, h * HALF // PER_COL : (h + 1) * HALF // PER_COL]
 
-        xt_plane = zeroed_plane(T, "xt_plane")
-        w_plane = zeroed_plane(R, "w_plane", "w_plane_board3")
+        xt_plane = zeroed_plane(T, "xt_plane", nc.gpsimd)
+        w_plane = zeroed_plane(R, "w_plane", nc.vector)
 
         w_stage = sb_tile([4, QUADS, R // 4], I32, "w_stage")
         nc.sync.dma_start(w_stage[:], w_scales[0].bitcast(I32).rearrange("(q r) c -> r q c", r=4))
         idx = load_list(offs, "idx")
         xt_table = sb_tile([P, T], U16, "xt_table")
-        nc.sync.dma_start(xt_table[:].bitcast(I32), xt_words[0].bitcast(I32))
-        w_raw = load_words(w_words, "w_raw", "w_raw_board2")
+        nc.scalar.dma_start(xt_table[:].bitcast(I32), xt_words[0].bitcast(I32))
+        w_raw = load_words(w_words, "w_raw", nc.scalar)
         load_plane(xt_plane, xt_scales)
         idx2 = load_list(offs2, "idx2")
 
@@ -79,66 +79,64 @@ def tile_list_ownsides_solo_further_scattered_kernel(
 
         w_codes, w_bytes = [], []
 
-        def deal_w(pair):
-            codes = sb_tile([P, 2, P], U32, "w_codes%d" % pair)
+        def deal_w_codes(first, count):
+            codes = sb_tile([P, count, P], U32, "w_codes%d" % first, "w_codes%d_next" % first)
             nc.scalar.copy(
                 codes[:].rearrange("p t m -> p m t"),
-                w_raw[:].rearrange("p (m t) -> p m t", t=PACK)[:, :, 2 * pair : 2 * pair + 2],
+                w_raw[:].rearrange("p (m t) -> p m t", t=PACK)[:, :, first : first + count],
             )
-            scales = sb_tile([P, 2, P], U8, "w_bytes%d" % pair)
-            nc.vector.tensor_copy(
-                scales[:], w_plane[:].rearrange("p (m t) -> p t m", t=PACK)[:, 2 * pair : 2 * pair + 2, :]
-            )
-            w_codes.extend([codes[:, 0, :], codes[:, 1, :]])
-            w_bytes.extend([scales[:, 0, :], scales[:, 1, :]])
+            w_codes.extend([codes[:, t, :] for t in range(count)])
 
-        slot_words = sb_tile([P, J], U16, "slot_words")
-        slot_bytes = sb_tile([P, J], U8, "slot_bytes")
+        def deal_w_bytes(first, count):
+            scales = sb_tile([P, count, P], U8, "w_bytes%d" % first, "w_bytes%d_next" % first)
+            nc.vector.tensor_copy(
+                scales[:], w_plane[:].rearrange("p (m t) -> p t m", t=PACK)[:, first : first + count, :]
+            )
+            w_bytes.extend([scales[:, t, :] for t in range(count)])
+
         hidden = [sb_tile([P, J], F32, "hidden%d" % t, "hidden%d_next" % t) for t in range(PACK)]
 
-        def gather_slots(h):
-            cols = slice(h * HALF, (h + 1) * HALF)
-            nc.vector.tensor_copy(slot_words[:, cols], xt_table[:].indirect(list_half(idx, h)))
-            nc.vector.tensor_copy(slot_bytes[:, cols], xt_plane[:].indirect(list_half(idx, h)))
-
-        def first_stage(t, cols, offsets, bank):
-            acc = psum.tile([P, cols.stop - cols.start], F32, name="acc_a%d_%d" % (t, cols.start), tag=bank)
-            nc.tensor.matmul_mx(
-                acc[:], lhsT=w_codes[t].bitcast(E5M2), lhsT_scale=w_bytes[t],
-                rhs=slot_words[:, cols].bitcast(E2M1), rhs_scale=slot_bytes[:, cols], start=True, stop=True,
-            )
-            nc.vector.tensor_copy(hidden[t][:, cols], acc[:])
-            nc.scalar.activation(boards[t][:].indirect(offsets), hidden[t][:, cols], COPY)
-
-        deal_w(0)
+        deal_w_codes(0, 1)
+        deal_w_bytes(0, 1)
         for h in range(2):
-            gather_slots(h)
-            for t in range(2):
-                first_stage(t, slice(h * HALF, (h + 1) * HALF), list_half(idx2, h), "bank%d" % (2 * h + t))
-        deal_w(1)
-        boards.append(sb_tile([P, C], F32, "board2", "w_raw_board2"))
-        boards.append(sb_tile([P, C], F32, "board3", "w_plane_board3"))
-        for t in range(2, PACK):
-            nc.gpsimd.memset(boards[t][:], 0.0)
-            first_stage(t, slice(0, J), idx2[:], "bank%d" % (2 + t))
+            cols = slice(h * HALF, (h + 1) * HALF)
+            slot_words = sb_tile([P, HALF], U16, "slot_words%d" % h, "slot_words")
+            slot_bytes = sb_tile([P, HALF], U8, "slot_bytes%d" % h, "slot_bytes")
+            nc.vector.tensor_copy(slot_words[:], xt_table[:].indirect(list_half(idx, h)))
+            nc.vector.tensor_copy(slot_bytes[:], xt_plane[:].indirect(list_half(idx, h)))
+            if h == 0:
+                deal_w_codes(1, 3)
+                deal_w_bytes(1, 3)
+                boards.append(sb_tile([P, C], F32, "board2", "w_raw"))
+                boards.append(sb_tile([P, C], F32, "board3", "w_plane"))
+                for t in range(2, PACK):
+                    nc.gpsimd.memset(boards[t][:], 0.0)
+            for t in range(PACK):
+                acc = psum.tile([P, HALF], F32, name="acc_a%d_%d" % (t, h), tag="bank%d" % (PACK * h + t))
+                nc.tensor.matmul_mx(
+                    acc[:], lhsT=w_codes[t].bitcast(E5M2), lhsT_scale=w_bytes[t],
+                    rhs=slot_words[:].bitcast(E2M1), rhs_scale=slot_bytes[:], start=True, stop=True,
+                )
+                nc.vector.tensor_copy(hidden[t][:, cols], acc[:])
+                nc.scalar.activation(boards[t][:].indirect(list_half(idx2, h)), hidden[t][:, cols], COPY)
 
         idx3 = load_list(offs3, "idx3")
-        sa_t = sb_tile([P, PACK], F32, "sa_t", "sa_picked1")
+        sa_t = sb_tile([P, PACK], F32, "sa_t")
         nc.sync.dma_start(sa_t[:], sa.rearrange("(p t) o -> p (t o)", t=PACK))
         idx5 = load_list(offs5, "idx5")
-        ws_codes = load_words(ws_words, "ws_codes")
-        ws_plane = zeroed_plane(N, "ws_plane")
+        ws_codes = load_words(ws_words, "ws_codes", nc.sync)
+        ws_plane = zeroed_plane(N, "ws_plane", nc.vector)
         load_plane(ws_plane, ws_scales)
         idx4 = load_list(offs4, "idx4")
         sb_t = sb_tile([P, PACK], F32, "sb_t")
         nc.sync.dma_start(sb_t[:], sb.rearrange("(p t) o -> p (t o)", t=PACK))
-        wb_codes = load_words(wb_words, "wb_codes")
-        wb_plane = zeroed_plane(N, "wb_plane")
+        wb_codes = load_words(wb_words, "wb_codes", nc.sync)
+        wb_plane = zeroed_plane(N, "wb_plane", nc.vector)
         load_plane(wb_plane, wb_scales)
         idx6 = load_list(offs6, "idx6")
 
-        short_words = sb_tile([P, D], U16, "short_words")
-        short_bytes = sb_tile([P, D], U8, "short_bytes")
+        short_words = sb_tile([P, D], U16, "short_words", "w_codes1_next")
+        short_bytes = sb_tile([P, D], U8, "short_bytes", "w_bytes1_next")
         nc.vector.tensor_copy(short_words[:], xt_table[:].indirect(idx5[:]))
         nc.vector.tensor_copy(short_bytes[:], xt_plane[:].indirect(idx5[:]))
 
@@ -158,14 +156,16 @@ def tile_list_ownsides_solo_further_scattered_kernel(
             pages.append(sb_tile([P, E], F32, "page%d" % n, "hidden%d_next" % n))
             nc.gpsimd.memset(pages[n][:], 0.0)
 
-        picked = [sb_tile([P, PACK, HALF], BF16, "picked0"), sb_tile([P, PACK, HALF], BF16, "picked1", "sa_picked1")]
+        picked = [sb_tile([P, PACK, HALF], BF16, "picked0", "hidden2_next"), sb_tile([P, PACK, HALF], BF16, "picked1", "hidden3_next")]
         for h, (places, weight) in enumerate(((idx3, sa_t), (idx4, sb_t))):
             for t in range(PACK):
                 nc.scalar.activation(
                     picked[h][:, t, :], boards[t][:].indirect(places[:]), COPY, scale=weight[:, t : t + 1]
                 )
 
+        results = [sb_tile([P, D], F32, "result%d" % n) for n in range(N // P)]
         for h in range(2):
+            cols = slice(h * HALF, (h + 1) * HALF)
             woven = sb_tile([P, HALF, PACK], BF16, "woven%d" % h, "woven")
             nc.vector.tensor_copy(woven[:], picked[h][:].rearrange("p t d -> p d t"))
             hid_codes = sb_tile([P, HALF], U32, "hid_codes%d" % h)
@@ -177,14 +177,15 @@ def tile_list_ownsides_solo_further_scattered_kernel(
                     sums[h, n][:], lhsT=wb_codes[:, rows].bitcast(E4M3), lhsT_scale=wb_plane[:, rows],
                     rhs=hid_codes[:].bitcast(E5M2), rhs_scale=hid_bytes[:], start=False, stop=True,
                 )
+            if h == 0:
+                nc.scalar.copy(results[0][:, cols], sums[h, 0][:])
+            else:
+                nc.vector.tensor_copy(results[0][:, cols], sums[h, 0][:])
+            nc.scalar.activation(pages[0][:].indirect(list_half(idx6, h)), results[0][:, cols], COPY)
 
         for h in range(2):
-            result0 = sb_tile([P, HALF], F32, "result0_%d" % h)
-            nc.scalar.copy(result0[:], sums[h, 0][:])
-            nc.scalar.activation(pages[0][:].indirect(list_half(idx6, h)), result0[:], COPY)
-            result1 = sb_tile([P, HALF], F32, "result1_%d" % h)
-            nc.vector.tensor_copy(result1[:], sums[h, 1][:])
-            nc.vector.tensor_copy(pages[1][:].indirect(list_half(idx6, h)), result1[:])
+            nc.vector.tensor_copy(results[1][:, h * HALF : (h + 1) * HALF], sums[h, 1][:])
+        nc.vector.tensor_copy(pages[1][:].indirect(idx6[:]), results[1][:])
 
         nc.scalar.dma_start(out[0:P, :], pages[0][:])
         nc.sync.dma_start(out[P : 2 * P, :], pages[1][:])

@@ -70,7 +70,7 @@ def tile_list_ownsides_solo_further_scattered_kernel(
         load_plane(xt_plane, xt_scales)
         idx2 = load_list(offs2, "idx2")
 
-        boards = [sb_tile([P, C], F32, "board0"), sb_tile([P, C], F32, "board1")]
+        boards = [sb_tile([P, C], F32, "board%d" % t) for t in range(PACK - 1)]
         for board in boards:
             nc.vector.memset(board[:], 0.0)
 
@@ -87,8 +87,8 @@ def tile_list_ownsides_solo_further_scattered_kernel(
             )
             w_codes.extend([codes[:, t, :] for t in range(count)])
 
-        def deal_w_bytes(first, count):
-            scales = sb_tile([P, count, P], U8, "w_bytes%d" % first, "w_bytes%d_next" % first)
+        def deal_w_bytes(first, count, tag):
+            scales = sb_tile([P, count, P], U8, "w_bytes%d" % first, tag)
             nc.vector.tensor_copy(
                 scales[:], w_plane[:].rearrange("p (m t) -> p t m", t=PACK)[:, first : first + count, :]
             )
@@ -97,7 +97,7 @@ def tile_list_ownsides_solo_further_scattered_kernel(
         hidden = [sb_tile([P, J], F32, "hidden%d" % t, "hidden%d_next" % t) for t in range(PACK)]
 
         deal_w_codes(0, 1)
-        deal_w_bytes(0, 1)
+        deal_w_bytes(0, 2, "w_bytes0")
         for h in range(2):
             cols = slice(h * HALF, (h + 1) * HALF)
             slot_words = sb_tile([P, HALF], U16, "slot_words%d" % h, "slot_words")
@@ -106,11 +106,9 @@ def tile_list_ownsides_solo_further_scattered_kernel(
             nc.vector.tensor_copy(slot_bytes[:], xt_plane[:].indirect(list_half(idx, h)))
             if h == 0:
                 deal_w_codes(1, 3)
-                deal_w_bytes(1, 3)
-                boards.append(sb_tile([P, C], F32, "board2", "w_raw"))
+                deal_w_bytes(2, 2, "w_raw")
                 boards.append(sb_tile([P, C], F32, "board3", "w_plane"))
-                for t in range(2, PACK):
-                    nc.gpsimd.memset(boards[t][:], 0.0)
+                nc.gpsimd.memset(boards[3][:], 0.0)
             for t in range(PACK):
                 acc = psum.tile([P, HALF], F32, name="acc_a%d_%d" % (t, h), tag="bank%d" % (PACK * h + t))
                 nc.tensor.matmul_mx(
@@ -125,18 +123,18 @@ def tile_list_ownsides_solo_further_scattered_kernel(
         nc.sync.dma_start(sa_t[:], sa.rearrange("(p t) o -> p (t o)", t=PACK))
         idx5 = load_list(offs5, "idx5")
         ws_codes = load_words(ws_words, "ws_codes", nc.sync)
-        ws_plane = zeroed_plane(N, "ws_plane", nc.vector)
+        ws_plane = zeroed_plane(N, "ws_plane", nc.gpsimd)
         load_plane(ws_plane, ws_scales)
         idx4 = load_list(offs4, "idx4")
         sb_t = sb_tile([P, PACK], F32, "sb_t")
         nc.sync.dma_start(sb_t[:], sb.rearrange("(p t) o -> p (t o)", t=PACK))
         wb_codes = load_words(wb_words, "wb_codes", nc.sync)
-        wb_plane = zeroed_plane(N, "wb_plane", nc.vector)
+        wb_plane = zeroed_plane(N, "wb_plane", nc.gpsimd)
         load_plane(wb_plane, wb_scales)
         idx6 = load_list(offs6, "idx6")
 
         short_words = sb_tile([P, D], U16, "short_words", "w_codes1_next")
-        short_bytes = sb_tile([P, D], U8, "short_bytes", "w_bytes1_next")
+        short_bytes = sb_tile([P, D], U8, "short_bytes", "w_raw")
         nc.vector.tensor_copy(short_words[:], xt_table[:].indirect(idx5[:]))
         nc.vector.tensor_copy(short_bytes[:], xt_plane[:].indirect(idx5[:]))
 
@@ -167,7 +165,8 @@ def tile_list_ownsides_solo_further_scattered_kernel(
         for h in range(2):
             cols = slice(h * HALF, (h + 1) * HALF)
             woven = sb_tile([P, HALF, PACK], BF16, "woven%d" % h, "woven")
-            nc.vector.tensor_copy(woven[:], picked[h][:].rearrange("p t d -> p d t"))
+            for part in (slice(0, 2), slice(2, PACK)):
+                nc.vector.tensor_copy(woven[:, :, part], picked[h][:, part, :].rearrange("p t d -> p d t"))
             hid_codes = sb_tile([P, HALF], U32, "hid_codes%d" % h)
             hid_bytes = sb_tile([P, HALF], U8, "hid_bytes%d" % h)
             nc.vector.quantize_mx(hid_codes[:].bitcast(E5M2), hid_bytes[:], woven[:].rearrange("p d t -> p (d t)"))

@@ -2,7 +2,7 @@ from contextlib import ExitStack
 
 import concourse.mybir as mybir
 
-K, T, J, R, C, O, U, D, N, E = 512, 1024, 256, 512, 512, 128, 128, 256, 256, 1024
+K, T, J, R, C, D, N, E = 512, 1024, 256, 512, 512, 256, 256, 1024
 FLOPS = 2 * K * R * J + 2 * R * N * D + 2 * K * N * D
 
 F32 = mybir.dt.float32
@@ -19,6 +19,9 @@ COPY = mybir.ActivationFunctionType.Copy
 P = 128
 PACK = 4
 QUADS = 4
+QUAD = 32
+LIVE = 4
+WORD = 4
 HALF = 128
 PER_COL = 16
 
@@ -33,7 +36,7 @@ def tile_list_ownsides_solo_further_scattered_kernel(
         keep = ctx.enter_context(tc.tile_pool(name="keep", bufs=1))
         psum = ctx.enter_context(tc.psum_pool(name="psum", bufs=1))
 
-        def sb_tile(shape, dtype, name, tag=None):
+        def sbuf(shape, dtype, name, tag=None):
             return keep.tile(shape, dtype, name=name, tag=tag or name, align_bytes=64)
 
         def load_list(src, name):
@@ -42,18 +45,21 @@ def tile_list_ownsides_solo_further_scattered_kernel(
             return dst
 
         def load_words(src, name, queue):
-            dst = sb_tile([P, src.shape[2]], U32, name)
+            dst = sbuf([P, src.shape[2]], U32, name)
             queue.dma_start(dst[:].bitcast(I32), src[0].rearrange("p n t -> p (n t)").bitcast(I32))
             return dst
 
         def zeroed_plane(width, name, engine):
-            plane = sb_tile([P, width], U8, name)
+            plane = sbuf([P, width], U8, name)
             engine.memset(plane[:].bitcast(I32), 0)
             return plane
 
+        def live_rows(plane, q):
+            return plane[QUAD * q : QUAD * q + LIVE, :].bitcast(I32)
+
         def load_plane(plane, src):
             for q in range(QUADS):
-                nc.sync.dma_start(plane[32 * q : 32 * q + 4, :].bitcast(I32), src[0, 4 * q : 4 * q + 4, :].bitcast(I32))
+                nc.sync.dma_start(live_rows(plane, q), src[0, LIVE * q : LIVE * (q + 1), :].bitcast(I32))
 
         def list_half(tile, h):
             return tile[:, h * HALF // PER_COL : (h + 1) * HALF // PER_COL]
@@ -61,26 +67,26 @@ def tile_list_ownsides_solo_further_scattered_kernel(
         xt_plane = zeroed_plane(T, "xt_plane", nc.gpsimd)
         w_plane = zeroed_plane(R, "w_plane", nc.vector)
 
-        w_stage = sb_tile([4, QUADS, R // 4], I32, "w_stage")
-        nc.sync.dma_start(w_stage[:], w_scales[0].bitcast(I32).rearrange("(q r) c -> r q c", r=4))
+        w_stage = sbuf([LIVE, QUADS, R // WORD], I32, "w_stage")
+        nc.sync.dma_start(w_stage[:], w_scales[0].bitcast(I32).rearrange("(q r) c -> r q c", r=LIVE))
         idx = load_list(offs, "idx")
-        xt_table = sb_tile([P, T], U16, "xt_table")
+        xt_table = sbuf([P, T], U16, "xt_table")
         nc.scalar.dma_start(xt_table[:].bitcast(I32), xt_words[0].bitcast(I32))
         w_raw = load_words(w_words, "w_raw", nc.scalar)
         load_plane(xt_plane, xt_scales)
         idx2 = load_list(offs2, "idx2")
 
-        boards = [sb_tile([P, C], F32, "board%d" % t) for t in range(PACK - 1)]
+        boards = [sbuf([P, C], F32, "board%d" % t) for t in range(PACK - 1)]
         for board in boards:
             nc.vector.memset(board[:], 0.0)
 
         for q in range(QUADS):
-            nc.vector.tensor_copy(w_plane[32 * q : 32 * q + 4, :].bitcast(I32), w_stage[0:4, q, :])
+            nc.vector.tensor_copy(live_rows(w_plane, q), w_stage[0:LIVE, q, :])
 
         w_codes, w_bytes = [], []
 
         def deal_w_codes(first, count):
-            codes = sb_tile([P, count, P], U32, "w_codes%d" % first, "w_codes%d_next" % first)
+            codes = sbuf([P, count, P], U32, "w_codes%d" % first, "w_codes%d_next" % first)
             nc.scalar.copy(
                 codes[:].rearrange("p t m -> p m t"),
                 w_raw[:].rearrange("p (m t) -> p m t", t=PACK)[:, :, first : first + count],
@@ -88,26 +94,26 @@ def tile_list_ownsides_solo_further_scattered_kernel(
             w_codes.extend([codes[:, t, :] for t in range(count)])
 
         def deal_w_bytes(first, count, tag):
-            scales = sb_tile([P, count, P], U8, "w_bytes%d" % first, tag)
+            scales = sbuf([P, count, P], U8, "w_bytes%d" % first, tag)
             nc.vector.tensor_copy(
                 scales[:], w_plane[:].rearrange("p (m t) -> p t m", t=PACK)[:, first : first + count, :]
             )
             w_bytes.extend([scales[:, t, :] for t in range(count)])
 
-        hidden = [sb_tile([P, J], F32, "hidden%d" % t, "hidden%d_next" % t) for t in range(PACK)]
+        hidden = [sbuf([P, J], F32, "hidden%d" % t, "hidden%d_next" % t) for t in range(PACK)]
 
         deal_w_codes(0, 1)
         deal_w_bytes(0, 2, "w_bytes0")
-        for h in range(2):
+        for h in range(J // HALF):
             cols = slice(h * HALF, (h + 1) * HALF)
-            slot_words = sb_tile([P, HALF], U16, "slot_words%d" % h, "slot_words")
-            slot_bytes = sb_tile([P, HALF], U8, "slot_bytes%d" % h, "slot_bytes")
+            slot_words = sbuf([P, HALF], U16, "slot_words%d" % h, "slot_words")
+            slot_bytes = sbuf([P, HALF], U8, "slot_bytes%d" % h, "slot_bytes")
             nc.vector.tensor_copy(slot_words[:], xt_table[:].indirect(list_half(idx, h)))
             nc.vector.tensor_copy(slot_bytes[:], xt_plane[:].indirect(list_half(idx, h)))
             if h == 0:
                 deal_w_codes(1, 3)
                 deal_w_bytes(2, 2, "w_raw")
-                boards.append(sb_tile([P, C], F32, "board3", "w_plane"))
+                boards.append(sbuf([P, C], F32, "board3", "w_plane"))
                 nc.gpsimd.memset(boards[3][:], 0.0)
             for t in range(PACK):
                 acc = psum.tile([P, HALF], F32, name="acc_a%d_%d" % (t, h), tag="bank%d" % (PACK * h + t))
@@ -119,31 +125,31 @@ def tile_list_ownsides_solo_further_scattered_kernel(
                 nc.scalar.activation(boards[t][:].indirect(list_half(idx2, h)), hidden[t][:, cols], COPY)
 
         idx3 = load_list(offs3, "idx3")
-        sa_t = sb_tile([P, PACK], F32, "sa_t")
-        nc.sync.dma_start(sa_t[:], sa.rearrange("(p t) o -> p (t o)", t=PACK))
+        sa_sets = sbuf([P, PACK], F32, "sa_t")
+        nc.sync.dma_start(sa_sets[:], sa.rearrange("(p t) o -> p (t o)", t=PACK))
         idx5 = load_list(offs5, "idx5")
         ws_codes = load_words(ws_words, "ws_codes", nc.sync)
         ws_plane = zeroed_plane(N, "ws_plane", nc.gpsimd)
         load_plane(ws_plane, ws_scales)
         idx4 = load_list(offs4, "idx4")
-        sb_t = sb_tile([P, PACK], F32, "sb_t")
-        nc.sync.dma_start(sb_t[:], sb.rearrange("(p t) o -> p (t o)", t=PACK))
+        sb_sets = sbuf([P, PACK], F32, "sb_t")
+        nc.sync.dma_start(sb_sets[:], sb.rearrange("(p t) o -> p (t o)", t=PACK))
         wb_codes = load_words(wb_words, "wb_codes", nc.sync)
         wb_plane = zeroed_plane(N, "wb_plane", nc.gpsimd)
         load_plane(wb_plane, wb_scales)
         idx6 = load_list(offs6, "idx6")
 
-        short_words = sb_tile([P, D], U16, "short_words", "w_codes1_next")
-        short_bytes = sb_tile([P, D], U8, "short_bytes", "w_raw")
+        short_words = sbuf([P, D], U16, "short_words", "w_codes1_next")
+        short_bytes = sbuf([P, D], U8, "short_bytes", "w_raw")
         nc.vector.tensor_copy(short_words[:], xt_table[:].indirect(idx5[:]))
         nc.vector.tensor_copy(short_bytes[:], xt_plane[:].indirect(idx5[:]))
 
         sums = {}
-        for h in range(2):
+        for h in range(D // HALF):
             cols = slice(h * HALF, (h + 1) * HALF)
             for n in range(N // P):
                 rows = slice(n * P, (n + 1) * P)
-                sums[h, n] = psum.tile([P, HALF], F32, name="acc_p%d_%d" % (h, n), tag="bank%d" % (2 * h + n))
+                sums[h, n] = psum.tile([P, HALF], F32, name="acc_p%d_%d" % (h, n), tag="bank%d" % (N // P * h + n))
                 nc.tensor.matmul_mx(
                     sums[h, n][:], lhsT=ws_codes[:, rows].bitcast(E4M3), lhsT_scale=ws_plane[:, rows],
                     rhs=short_words[:, cols].bitcast(E2M1), rhs_scale=short_bytes[:, cols], start=True, stop=False,
@@ -151,25 +157,30 @@ def tile_list_ownsides_solo_further_scattered_kernel(
 
         pages = []
         for n in range(N // P):
-            pages.append(sb_tile([P, E], F32, "page%d" % n, "hidden%d_next" % n))
+            pages.append(sbuf([P, E], F32, "page%d" % n, "hidden%d_next" % n))
             nc.gpsimd.memset(pages[n][:], 0.0)
 
-        picked = [sb_tile([P, PACK, HALF], BF16, "picked0", "hidden2_next"), sb_tile([P, PACK, HALF], BF16, "picked1", "hidden3_next")]
-        for h, (places, weight) in enumerate(((idx3, sa_t), (idx4, sb_t))):
+        picked = [sbuf([P, PACK, HALF], BF16, "picked%d" % h, "hidden%d_next" % (2 + h)) for h in range(D // HALF)]
+        for h, (places, weight) in enumerate(((idx3, sa_sets), (idx4, sb_sets))):
             for t in range(PACK):
                 nc.scalar.activation(
                     picked[h][:, t, :], boards[t][:].indirect(places[:]), COPY, scale=weight[:, t : t + 1]
                 )
 
-        results = [sb_tile([P, D], F32, "result%d" % n) for n in range(N // P)]
-        for h in range(2):
+        results = [sbuf([P, D], F32, "result%d" % n) for n in range(N // P)]
+        for h in range(D // HALF):
             cols = slice(h * HALF, (h + 1) * HALF)
-            woven = sb_tile([P, HALF, PACK], BF16, "woven%d" % h, "woven")
-            for part in (slice(0, 2), slice(2, PACK)):
-                nc.vector.tensor_copy(woven[:, :, part], picked[h][:, part, :].rearrange("p t d -> p d t"))
-            hid_codes = sb_tile([P, HALF], U32, "hid_codes%d" % h)
-            hid_bytes = sb_tile([P, HALF], U8, "hid_bytes%d" % h)
-            nc.vector.quantize_mx(hid_codes[:].bitcast(E5M2), hid_bytes[:], woven[:].rearrange("p d t -> p (d t)"))
+            woven = sbuf([P, HALF, PACK], BF16, "woven%d" % h, "woven")
+            nc.vector.tensor_copy(woven[:, :, 0:2], picked[h][:, 0:2, :].rearrange("p t d -> p d t"))
+            parts = (slice(0, HALF // 2), slice(HALF // 2, HALF))
+            for part in parts:
+                nc.vector.tensor_copy(woven[:, part, 2:PACK], picked[h][:, 2:PACK, part].rearrange("p t d -> p d t"))
+            hid_codes = sbuf([P, HALF], U32, "hid_codes%d" % h)
+            hid_bytes = sbuf([P, HALF], U8, "hid_bytes%d" % h)
+            for part in parts:
+                nc.vector.quantize_mx(
+                    hid_codes[:, part].bitcast(E5M2), hid_bytes[:, part], woven[:, part, :].rearrange("p d t -> p (d t)")
+                )
             for n in range(N // P):
                 rows = slice(n * P, (n + 1) * P)
                 nc.tensor.matmul_mx(
@@ -182,7 +193,7 @@ def tile_list_ownsides_solo_further_scattered_kernel(
                 nc.vector.tensor_copy(results[0][:, cols], sums[h, 0][:])
             nc.scalar.activation(pages[0][:].indirect(list_half(idx6, h)), results[0][:, cols], COPY)
 
-        for h in range(2):
+        for h in range(D // HALF):
             nc.vector.tensor_copy(results[1][:, h * HALF : (h + 1) * HALF], sums[h, 1][:])
         nc.vector.tensor_copy(pages[1][:].indirect(idx6[:]), results[1][:])
 

from contextlib import ExitStack

import concourse.mybir as mybir

K, T, J, R, C, D, N, E = 512, 1024, 256, 512, 512, 256, 256, 1024
FLOPS = 2 * K * R * J + 2 * R * N * D + 2 * K * N * D

F32 = mybir.dt.float32
BF16 = mybir.dt.bfloat16
I32 = mybir.dt.int32
U32 = mybir.dt.uint32
U16 = mybir.dt.uint16
U8 = mybir.dt.uint8
E4M3 = mybir.dt.float8_e4m3fn_x4
E5M2 = mybir.dt.float8_e5m2_x4
E2M1 = mybir.dt.float4_e2m1fn_x4
COPY = mybir.ActivationFunctionType.Copy

P = 128
PACK = 4
QUADS = 4
QUAD = 32
LIVE = 4
WORD = 4
HALF = 128
PER_COL = 16


def tile_list_ownsides_solo_further_scattered_kernel(
    tc, xt_words, xt_scales, w_words, w_scales, sa, sb, wb_words, wb_scales, ws_words, ws_scales,
    offs, offs2, offs3, offs4, offs5, offs6, out,
):
    nc = tc.nc
    with ExitStack() as ctx:
        lists = ctx.enter_context(tc.tile_pool(name="lists", bufs=1))
        keep = ctx.enter_context(tc.tile_pool(name="keep", bufs=1))
        psum = ctx.enter_context(tc.psum_pool(name="psum", bufs=1))

        def sbuf(shape, dtype, name, tag=None):
            return keep.tile(shape, dtype, name=name, tag=tag or name, align_bytes=64)

        def load_list(src, name):
            dst = lists.tile(list(src.shape), U16, name=name)
            nc.sync.dma_start(dst[:], src)
            return dst

        def load_words(src, name, queue):
            dst = sbuf([P, src.shape[2]], U32, name)
            queue.dma_start(dst[:].bitcast(I32), src[0].rearrange("p n t -> p (n t)").bitcast(I32))
            return dst

        def zeroed_plane(width, name, engine):
            plane = sbuf([P, width], U8, name)
            engine.memset(plane[:].bitcast(I32), 0)
            return plane

        def live_rows(plane, q):
            return plane[QUAD * q : QUAD * q + LIVE, :].bitcast(I32)

        def load_plane(plane, src):
            for q in range(QUADS):
                nc.sync.dma_start(live_rows(plane, q), src[0, LIVE * q : LIVE * (q + 1), :].bitcast(I32))

        def list_half(tile, h):
            return tile[:, h * HALF // PER_COL : (h + 1) * HALF // PER_COL]

        xt_plane = zeroed_plane(T, "xt_plane", nc.gpsimd)
        w_plane = zeroed_plane(R, "w_plane", nc.vector)

        w_stage = sbuf([LIVE, QUADS, R // WORD], I32, "w_stage")
        nc.sync.dma_start(w_stage[:], w_scales[0].bitcast(I32).rearrange("(q r) c -> r q c", r=LIVE))
        idx = load_list(offs, "idx")
        xt_table = sbuf([P, T], U16, "xt_table")
        nc.scalar.dma_start(xt_table[:].bitcast(I32), xt_words[0].bitcast(I32))
        w_raw = load_words(w_words, "w_raw", nc.scalar)
        load_plane(xt_plane, xt_scales)
        idx2 = load_list(offs2, "idx2")

        boards = [sbuf([P, C], F32, "board%d" % t) for t in range(PACK - 1)]
        for board in boards:
            nc.vector.memset(board[:], 0.0)

        for q in range(QUADS):
            nc.vector.tensor_copy(live_rows(w_plane, q), w_stage[0:LIVE, q, :])

        w_codes, w_bytes = [], []

        def deal_w_codes(first, count):
            codes = sbuf([P, count, P], U32, "w_codes%d" % first, "w_codes%d_next" % first)
            nc.scalar.copy(
                codes[:].rearrange("p t m -> p m t"),
                w_raw[:].rearrange("p (m t) -> p m t", t=PACK)[:, :, first : first + count],
            )
            w_codes.extend([codes[:, t, :] for t in range(count)])

        def deal_w_bytes(first, count, tag):
            scales = sbuf([P, count, P], U8, "w_bytes%d" % first, tag)
            nc.vector.tensor_copy(
                scales[:], w_plane[:].rearrange("p (m t) -> p t m", t=PACK)[:, first : first + count, :]
            )
            w_bytes.extend([scales[:, t, :] for t in range(count)])

        hidden = [sbuf([P, J], F32, "hidden%d" % t, "hidden%d_next" % t) for t in range(PACK)]

        deal_w_codes(0, 1)
        deal_w_bytes(0, 2, "w_bytes0")
        for h in range(J // HALF):
            cols = slice(h * HALF, (h + 1) * HALF)
            slot_words = sbuf([P, HALF], U16, "slot_words%d" % h, "slot_words")
            slot_bytes = sbuf([P, HALF], U8, "slot_bytes%d" % h, "slot_bytes")
            nc.vector.tensor_copy(slot_words[:], xt_table[:].indirect(list_half(idx, h)))
            nc.vector.tensor_copy(slot_bytes[:], xt_plane[:].indirect(list_half(idx, h)))
            if h == 0:
                deal_w_codes(1, 3)
                deal_w_bytes(2, 2, "w_raw")
                boards.append(sbuf([P, C], F32, "board3", "w_plane"))
                nc.gpsimd.memset(boards[3][:], 0.0)
            for t in range(PACK):
                acc = psum.tile([P, HALF], F32, name="acc_a%d_%d" % (t, h), tag="bank%d" % (PACK * h + t))
                nc.tensor.matmul_mx(
                    acc[:], lhsT=w_codes[t].bitcast(E5M2), lhsT_scale=w_bytes[t],
                    rhs=slot_words[:].bitcast(E2M1), rhs_scale=slot_bytes[:], start=True, stop=True,
                )
                nc.vector.tensor_copy(hidden[t][:, cols], acc[:])
                nc.scalar.activation(boards[t][:].indirect(list_half(idx2, h)), hidden[t][:, cols], COPY)

        idx3 = load_list(offs3, "idx3")
        sa_sets = sbuf([P, PACK], F32, "sa_t")
        nc.sync.dma_start(sa_sets[:], sa.rearrange("(p t) o -> p (t o)", t=PACK))
        idx5 = load_list(offs5, "idx5")
        ws_codes = load_words(ws_words, "ws_codes", nc.sync)
        ws_plane = zeroed_plane(N, "ws_plane", nc.gpsimd)
        load_plane(ws_plane, ws_scales)
        idx4 = load_list(offs4, "idx4")
        sb_sets = sbuf([P, PACK], F32, "sb_t")
        nc.sync.dma_start(sb_sets[:], sb.rearrange("(p t) o -> p (t o)", t=PACK))
        wb_codes = load_words(wb_words, "wb_codes", nc.sync)
        wb_plane = zeroed_plane(N, "wb_plane", nc.gpsimd)
        load_plane(wb_plane, wb_scales)
        idx6 = load_list(offs6, "idx6")

        short_words = sbuf([P, D], U16, "short_words", "w_codes1_next")
        short_bytes = sbuf([P, D], U8, "short_bytes", "w_raw")
        nc.vector.tensor_copy(short_words[:], xt_table[:].indirect(idx5[:]))
        nc.vector.tensor_copy(short_bytes[:], xt_plane[:].indirect(idx5[:]))

        sums = {}
        for h in range(D // HALF):
            cols = slice(h * HALF, (h + 1) * HALF)
            for n in range(N // P):
                rows = slice(n * P, (n + 1) * P)
                sums[h, n] = psum.tile([P, HALF], F32, name="acc_p%d_%d" % (h, n), tag="bank%d" % (N // P * h + n))
                nc.tensor.matmul_mx(
                    sums[h, n][:], lhsT=ws_codes[:, rows].bitcast(E4M3), lhsT_scale=ws_plane[:, rows],
                    rhs=short_words[:, cols].bitcast(E2M1), rhs_scale=short_bytes[:, cols], start=True, stop=False,
                )

        pages = []
        for n in range(N // P):
            pages.append(sbuf([P, E], F32, "page%d" % n, "hidden%d_next" % n))
            nc.gpsimd.memset(pages[n][:], 0.0)

        picked = [sbuf([P, PACK, HALF], BF16, "picked%d" % h, "hidden%d_next" % (2 + h)) for h in range(D // HALF)]
        for h, (places, weight) in enumerate(((idx3, sa_sets), (idx4, sb_sets))):
            for t in range(PACK):
                nc.scalar.activation(
                    picked[h][:, t, :], boards[t][:].indirect(places[:]), COPY, scale=weight[:, t : t + 1]
                )

        results = [sbuf([P, D], F32, "result%d" % n) for n in range(N // P)]
        for h in range(D // HALF):
            cols = slice(h * HALF, (h + 1) * HALF)
            woven = sbuf([P, HALF, PACK], BF16, "woven%d" % h, "woven")
            nc.vector.tensor_copy(woven[:, :, 0:2], picked[h][:, 0:2, :].rearrange("p t d -> p d t"))
            parts = (slice(0, HALF // 2), slice(HALF // 2, HALF))
            for part in parts:
                nc.vector.tensor_copy(woven[:, part, 2:PACK], picked[h][:, 2:PACK, part].rearrange("p t d -> p d t"))
            hid_codes = sbuf([P, HALF], U32, "hid_codes%d" % h)
            hid_bytes = sbuf([P, HALF], U8, "hid_bytes%d" % h)
            for part in parts:
                nc.vector.quantize_mx(
                    hid_codes[:, part].bitcast(E5M2), hid_bytes[:, part], woven[:, part, :].rearrange("p d t -> p (d t)")
                )
            for n in range(N // P):
                rows = slice(n * P, (n + 1) * P)
                nc.tensor.matmul_mx(
                    sums[h, n][:], lhsT=wb_codes[:, rows].bitcast(E4M3), lhsT_scale=wb_plane[:, rows],
                    rhs=hid_codes[:].bitcast(E5M2), rhs_scale=hid_bytes[:], start=False, stop=True,
                )
            if h == 0:
                nc.scalar.copy(results[0][:, cols], sums[h, 0][:])
            else:
                nc.vector.tensor_copy(results[0][:, cols], sums[h, 0][:])
            nc.scalar.activation(pages[0][:].indirect(list_half(idx6, h)), results[0][:, cols], COPY)

        for h in range(D // HALF):
            nc.vector.tensor_copy(results[1][:, h * HALF : (h + 1) * HALF], sums[h, 1][:])
        nc.vector.tensor_copy(pages[1][:].indirect(idx6[:]), results[1][:])

        nc.scalar.dma_start(out[0:P, :], pages[0][:])
        nc.sync.dma_start(out[P : 2 * P, :], pages[1][:])
